import numpy as np
import ml_dtypes


def mxq(x, axis, fmt="e4m3"):
    dtype, down = {"e4m3": (ml_dtypes.float8_e4m3fn, 7), "e5m2": (ml_dtypes.float8_e5m2, 14)}[fmt]
    v = np.moveaxis(np.asarray(x, np.float32).astype(ml_dtypes.bfloat16).astype(np.float64), axis, -1)
    blocks = v.reshape(v.shape[:-1] + (-1, 32))
    amax = np.abs(blocks).max(-1, keepdims=True)
    byte = np.maximum(np.where(amax > 0, np.frexp(amax)[1] - 1 + 127, 0) - down, 1)
    scale = np.exp2(byte - 127.0)
    codes = (blocks / scale).astype(np.float32).astype(dtype).astype(np.float64)
    return np.moveaxis((codes * scale).reshape(v.shape), -1, axis)


WIDE = False


def mx_kscale(k):
    if not WIDE:
        return np.ones(k)
    levels = np.array([10, -10, 5, -5, 0])
    if k % 512:
        return np.exp2(np.random.permutation(np.resize(levels, k // 32))).repeat(32)
    a = np.empty((k // 512, 16))
    for p in range(k // 512):
        a[p, :8] = np.random.permutation(np.resize(levels, 8))
        for g in range(8):
            far = levels[np.abs(levels - a[p, g]) >= 10]
            a[p, g + 8] = far[np.random.randint(len(far))]
    return np.exp2(a.ravel()).repeat(32)


def f64(x):
    return np.asarray(x).astype(np.float64)


def striped(idx):
    return np.tile(idx.reshape(-1, 16).T, (8, 1)).astype(np.uint16)


def unstriped(offs):
    return offs[:16].T.reshape(-1).astype(np.int64)


def striped8(idx):
    return np.concatenate([x.reshape(-1, 16).T for x in idx]).astype(np.uint16)


def runs(offs, k):
    lists = np.stack([offs[16 * r : 16 * r + 16].T.reshape(-1) for r in range(8)]).astype(np.int64)
    return lists[np.arange(k) % 512 // 64]


def pack_weight(w):
    k, n = w.shape
    w = f64(np.asarray(w, np.float32).astype(ml_dtypes.bfloat16)).reshape(k // 32, 32, n)
    amax = np.abs(w).max(1)
    byte = np.clip(np.where(amax > 0, np.frexp(amax)[1] - 1 + 127 - 7, 1), 1, 254)
    scaled = (w * np.exp2(127.0 - byte)[:, None, :]).reshape(k, n).astype(np.float32)
    words = np.ascontiguousarray(scaled.reshape(k // 512, 128, 4, n).transpose(0, 1, 3, 2)).astype(ml_dtypes.float8_e4m3fn).view(np.uint8)
    return words, np.ascontiguousarray(byte.astype(np.uint8).reshape(k // 512, 16, n))


def unpack_weight(words, scales):
    g, p, n, _ = words.shape
    vals = np.ascontiguousarray(words).view(ml_dtypes.float8_e4m3fn).astype(np.float64) * np.repeat(np.exp2(scales.astype(np.float64) - 127.0), 8, axis=1)[..., None]
    return vals.transpose(0, 1, 3, 2).reshape(g * 512, n)


E2M1 = np.array([0.0, 0.5, 1.0, 1.5, 2.0, 3.0, 4.0, 6.0, -0.0, -0.5, -1.0, -1.5, -2.0, -3.0, -4.0, -6.0])


def pack_fp4(w):
    k, n = w.shape
    w = f64(np.asarray(w, np.float32).astype(ml_dtypes.bfloat16)).reshape(k // 32, 32, n)
    amax = np.abs(w).max(1)
    mant, ex = np.frexp(amax / 6.0)
    byte = np.clip(np.where(amax > 0, np.where(mant > 0.5, ex, ex - 1) + 127, 1), 1, 254)
    scaled = (w * np.exp2(127.0 - byte)[:, None, :]).reshape(k, n).astype(np.float32)
    c = np.ascontiguousarray(scaled.reshape(k // 512, 128, 4, n).transpose(0, 1, 3, 2)).astype(ml_dtypes.float4_e2m1fn).view(np.uint8) & 0xF
    words = (c[..., 0::2] | (c[..., 1::2] << 4)).reshape(k // 512, 128, 2 * n)
    return np.ascontiguousarray(words), np.ascontiguousarray(byte.astype(np.uint8).reshape(k // 512, 16, n))


def unpack_fp4(words, scales):
    g, _, n = scales.shape
    words = np.ascontiguousarray(words).reshape(g, 128, n, 2)
    nib = np.empty((g, 128, n, 4), np.uint8)
    nib[..., 0::2] = words & 0xF
    nib[..., 1::2] = words >> 4
    vals = E2M1[nib] * np.repeat(np.exp2(scales.astype(np.float64) - 127.0), 8, axis=1)[..., None]
    return vals.transpose(0, 1, 3, 2).reshape(g * 512, n)


def sigmoid(v):
    return 1.0 / (1.0 + np.exp(-np.maximum(v, -700.0)))

def planes(y):
    n, m = y.shape
    v = y.astype(np.float32).astype(ml_dtypes.bfloat16).astype(np.float64).reshape(n // 32, 32, m)
    top = np.abs(v).max(1)
    byte = np.clip(np.where(top > 0, np.frexp(top)[1] - 1 + 127 - 7, 1), 1, 254)
    codes = (v * np.exp2(127.0 - byte)[:, None, :]).reshape(n, m).astype(np.float32).astype(ml_dtypes.float8_e4m3fn).view(np.uint8)
    words = codes.reshape(n // 512, 128, 4, m).transpose(0, 1, 3, 2)
    return np.ascontiguousarray(words), np.ascontiguousarray(byte.astype(np.uint8).reshape(n // 512, 16, m))


K, T, S, N, H = 512, 2048, 512, 512, 512


def setup_inputs():
    n = np.random.standard_normal
    s = mx_kscale(K)[:, None]
    u = mx_kscale(S)
    packed_xT = pack_weight(n((K, T)) * s)
    packed_w1 = pack_fp4(n((S, N)) / np.sqrt(S) / u[:, None])
    return {
        "x_words": packed_xT[0],
        "x_scales": packed_xT[1],
        "wa": (n((K, H)) / np.sqrt(K) / s).astype(np.float32),
        "gt": (np.random.uniform(0.5, 1.5, (S, 1)) * u[:, None]).astype(np.float32),
        "w1_words": packed_w1[0],
        "w1_scales": packed_w1[1],
        "offs": striped(np.random.permutation(T)[:S]),
        "n1": striped8(np.stack([np.random.permutation(H) for _ in range(8)])),
        "n2": striped8(np.stack([np.random.permutation(H) for _ in range(8)])),
        "n3": striped8(np.stack([np.random.permutation(H) for _ in range(8)])),
    }


def reference(x_words, x_scales, wa, gt, w1_words, w1_scales, offs, n1, n2, n3):
    xq = unpack_weight(x_words, x_scales)[:, unstriped(offs)]
    y = xq.T @ mxq(f64(wa), 0, "e4m3")
    pa = y[np.arange(S)[:, None], runs(n1, S)]
    kr = np.exp(-0.5 * ((y - pa) ** 2))
    pb = y[np.arange(S)[:, None], runs(n2, S)]
    kr2 = np.exp(-0.5 * ((y - pb) ** 2))
    z = f64(gt) * ((kr * pa + kr2 * pb) / (kr + kr2 + 0.5))
    h = unpack_fp4(w1_words, w1_scales).T @ mxq(z, 0, "e4m3")
    out_0 = h * (sigmoid(h[np.arange(N)[:, None], runs(n3, N)]))
    return (out_0,) + planes(out_0)

@@ -1,0 +1,228 @@
+from contextlib import ExitStack
+
+import concourse.mybir as mybir
+
+K, T, S, N, H = 512, 2048, 512, 512, 512
+FLOPS = 2 * K * S * H + 2 * S * N * H
+
+F32 = mybir.dt.float32
+BF16 = mybir.dt.bfloat16
+I32 = mybir.dt.int32
+U32 = mybir.dt.uint32
+U16 = mybir.dt.uint16
+U8 = mybir.dt.uint8
+FP8X4 = mybir.dt.float8_e4m3fn_x4
+FP4X4 = mybir.dt.float4_e2m1fn_x4
+ACT = mybir.ActivationFunctionType
+ALU = mybir.AluOpType
+
+P = 128
+PACK = 4
+HALF = H // 2
+LANES = 16
+
+
+def tile_picked_tokkerngate_none_po_kernel(
+    tc, x_words, x_scales, wa, gt, w1_words, w1_scales, offs, n1, n2, n3, out_0, out_1, out_2
+):
+    nc = tc.nc
+    halves = [slice(h * HALF, (h + 1) * HALF) for h in range(2)]
+    quarters = [slice(i * P, (i + 1) * P) for i in range(4)]
+    list_halves = [slice(h * HALF // LANES, (h + 1) * HALF // LANES) for h in range(2)]
+
+    with ExitStack() as ctx:
+        sb = ctx.enter_context(tc.tile_pool(name="sb", bufs=1))
+        ps = ctx.enter_context(tc.psum_pool(name="ps", bufs=1))
+
+        def tile(shape, dtype, name):
+            return sb.tile(shape, dtype, name=name, align_bytes=64)
+
+        offs_sb = tile([P, S // LANES], U16, "offs_sb")
+        n1_sb = tile([P, H // LANES], U16, "n1_sb")
+        n2_sb = tile([P, H // LANES], U16, "n2_sb")
+        n3_sb = tile([P, H // LANES], U16, "n3_sb")
+        xw_all = tile([P, T], I32, "xw_all")
+        xs_all = tile([P, T], U8, "xs_all")
+        w1w_raw = tile([P, 2 * N], U8, "w1w_raw")
+        w1s_raw = tile([P, N], U8, "w1s_raw")
+        wa_cuts = [slice(0, 256), slice(256, 384), slice(384, 512)]
+        wa_raw = [tile([P, PACK, c.stop - c.start], F32, f"wa_raw{c.start}") for c in wa_cuts]
+        gt_sb = tile([P, PACK], F32, "gt_sb")
+
+        nc.vector.memset(xs_all[:].bitcast(I32), 0)
+        nc.vector.memset(w1s_raw[:].bitcast(I32), 0)
+
+        nc.sync.dma_start(offs_sb[:], offs)
+        for q in range(4):
+            nc.sync.dma_start(
+                xs_all[32 * q : 32 * q + 4, :].bitcast(I32), x_scales[0, 4 * q : 4 * q + 4, :].bitcast(I32)
+            )
+        nc.sync.dma_start(xw_all[:], x_words[0].rearrange("p c r -> p (c r)").bitcast(I32))
+        wa_rows = wa.rearrange("(p j) c -> p j c", j=PACK)
+        for raw, c in zip(wa_raw, wa_cuts):
+            nc.sync.dma_start(raw[:], wa_rows[:, :, c])
+        nc.sync.dma_start(n1_sb[:], n1)
+        nc.sync.dma_start(n2_sb[:], n2)
+        nc.sync.dma_start(w1w_raw[:].bitcast(I32), w1_words[0].bitcast(I32))
+        for q in range(4):
+            nc.sync.dma_start(
+                w1s_raw[32 * q : 32 * q + 4, :].bitcast(I32), w1_scales[0, 4 * q : 4 * q + 4, :].bitcast(I32)
+            )
+        nc.sync.dma_start(gt_sb[:], gt.rearrange("(p t) o -> p (t o)", t=PACK))
+        nc.sync.dma_start(n3_sb[:], n3)
+
+        xs_picked = tile([P, S], U8, "xs_picked")
+        xs_dealt = tile([P, S], U8, "xs_dealt")
+        xw_dealt = tile([P, S], U32, "xw_dealt")
+        nc.vector.tensor_copy(xs_picked[:], xs_all[:].indirect(offs_sb[:]))
+        nc.vector.tensor_copy(
+            xw_dealt[:].rearrange("p (t m) -> p m t", t=PACK), xw_all[:].bitcast(U32).indirect(offs_sb[:])
+        )
+        nc.vector.tensor_copy(
+            xs_dealt[:].rearrange("p (t m) -> p t m", t=PACK), xs_picked[:].rearrange("p (m t) -> p t m", t=PACK)
+        )
+
+        def woven(ap):
+            return ap.rearrange("p (c i t) -> p c t i", i=4, t=PACK)
+
+        def planar(ap):
+            return ap.rearrange("p t (c i) -> p c t i", i=4)
+
+        wa_bf = [tile([P, (c.stop - c.start) * PACK], BF16, f"wa_bf{c.start}") for c in wa_cuts]
+        wa_codes = tile([P, H], U32, "wa_codes")
+        wa_scales = tile([P, H], U8, "wa_scales")
+        y_ps = [ps.tile([P, H], F32, name=f"y_ps{t}") for t in range(PACK)]
+        for i, c in enumerate(wa_cuts):
+            if i < len(wa_cuts) - 1:
+                nc.scalar.copy(woven(wa_bf[i][:]), planar(wa_raw[i][:]))
+            else:
+                nc.vector.tensor_copy(woven(wa_bf[i][:]), planar(wa_raw[i][:]))
+            nc.vector.quantize_mx(out=wa_codes[:, c].bitcast(FP8X4), scales=wa_scales[:, c], in_=wa_bf[i][:])
+            for t in range(PACK):
+                cols = slice(t * P, (t + 1) * P)
+                nc.tensor.matmul_mx(
+                    out=y_ps[t][:, c],
+                    lhsT=xw_dealt[:, cols].bitcast(FP8X4),
+                    lhsT_scale=xs_dealt[:, cols],
+                    rhs=wa_codes[:, c].bitcast(FP8X4),
+                    rhs_scale=wa_scales[:, c],
+                    start=True,
+                    stop=True,
+                )
+
+        w1w_dealt = tile([P, 2 * N], U8, "w1w_dealt")
+        w1s_dealt = tile([P, N], U8, "w1s_dealt")
+        nc.vector.tensor_copy(
+            w1w_dealt[:].rearrange("p (t m b) -> p t m b", t=PACK, b=2),
+            w1w_raw[:].rearrange("p (m t b) -> p t m b", t=PACK, b=2),
+        )
+        nc.vector.tensor_copy(
+            w1s_dealt[:].rearrange("p (t m) -> p t m", t=PACK), w1s_raw[:].rearrange("p (m t) -> p t m", t=PACK)
+        )
+
+        y_sb = [tile([P, H], F32, f"y_sb{t}") for t in range(PACK)]
+        near = [tile([P, 2, H], F32, f"near{t}") for t in range(PACK)]
+        diff = [tile([P, 2, H], F32, f"diff{t}") for t in range(PACK)]
+        sq = [tile([P, 2, H], F32, f"sq{t}") for t in range(PACK)]
+        kern = [tile([P, 2, H], F32, f"kern{t}") for t in range(PACK)]
+        prod = [tile([P, 2, H], F32, f"prod{t}") for t in range(PACK)]
+        den = tile([P, PACK, H], F32, "den")
+        den_sq = tile([P, PACK, H], F32, "den_sq")
+        inv = tile([P, PACK, H], F32, "inv")
+        num = tile([P, PACK, H], F32, "num")
+
+        for t in range(PACK):
+            nc.scalar.copy(y_sb[t][:], y_ps[t][:])
+        for t in range(PACK):
+            for e, lst in enumerate((n1_sb, n2_sb)):
+                for h in range(2):
+                    nc.vector.tensor_copy(near[t][:, e, halves[h]], y_sb[t][:].indirect(lst[:, list_halves[h]]))
+            for e in range(2):
+                nc.vector.tensor_tensor(diff[t][:, e, :], y_ps[t][:], near[t][:, e, :], ALU.subtract)
+            for e in range(2):
+                nc.scalar.activation(sq[t][:, e, :], diff[t][:, e, :], ACT.Square)
+            for e in range(2):
+                nc.scalar.activation(kern[t][:, e, :], sq[t][:, e, :], ACT.Exp, scale=-0.5)
+
+        def denominator(t):
+            nc.vector.scalar_tensor_tensor(den[:, t, :], kern[t][:, 0, :], 0.5, kern[t][:, 1, :], ALU.add, ALU.add)
+            nc.scalar.activation(den_sq[:, t, :], den[:, t, :], ACT.Square)
+
+        def products(t):
+            nc.vector.scalar_tensor_tensor(
+                prod[t][:], kern[t][:], gt_sb[:, t : t + 1], near[t][:], ALU.mult, ALU.mult
+            )
+
+        def numerator(t):
+            nc.vector.tensor_tensor(num[:, t, :], prod[t][:, 0, :], prod[t][:, 1, :], ALU.add)
+
+        for t in range(PACK - 1):
+            denominator(t)
+        products(0)
+        denominator(PACK - 1)
+        for t in range(1, PACK):
+            products(t)
+            numerator(t - 1)
+        for c in quarters:
+            nc.scalar.activation(inv[:, :, c], den_sq[:, :, c], ACT.Abs_reciprocal_sqrt)
+        numerator(PACK - 1)
+
+        z_bf = [tile([P, P * PACK], BF16, f"z_bf{i}") for i in range(4)]
+        z_codes = tile([P, H], U32, "z_codes")
+        z_scales = tile([P, H], U8, "z_scales")
+        h_ps = [ps.tile([P, PACK, P], F32, name=f"h_ps{i}") for i in range(4)]
+        window = [tile([P, H], F32, f"window{t}") for t in range(PACK)]
+
+        def divide(i):
+            c = quarters[i]
+            nc.vector.tensor_tensor(woven(z_bf[i][:]), planar(num[:, :, c]), planar(inv[:, :, c]), ALU.mult)
+
+        def second_product(i):
+            c = quarters[i]
+            nc.vector.quantize_mx(out=z_codes[:, c].bitcast(FP8X4), scales=z_scales[:, c], in_=z_bf[i][:])
+            for t in range(PACK):
+                nc.tensor.matmul_mx(
+                    out=h_ps[i][:, t, :],
+                    lhsT=w1w_dealt[:, 2 * t * P : 2 * (t + 1) * P].bitcast(FP4X4),
+                    lhsT_scale=w1s_dealt[:, t * P : (t + 1) * P],
+                    rhs=z_codes[:, c].bitcast(FP8X4),
+                    rhs_scale=z_scales[:, c],
+                    start=True,
+                    stop=True,
+                )
+            nc.scalar.activation(window[0][:, c], h_ps[i][:, 0, :], ACT.Sigmoid)
+            for t in range(1, PACK):
+                nc.scalar.copy(window[t][:, c], h_ps[i][:, t, :])
+
+        divide(0)
+        for i in range(1, 4):
+            divide(i)
+            second_product(i - 1)
+        second_product(3)
+
+        gate = tile([P, PACK, H], F32, "gate")
+        res = tile([P, PACK, H], F32, "res")
+        res_bf = tile([P, H * PACK], BF16, "res_bf")
+        res_codes = tile([P, H], I32, "res_codes")
+        res_scales = tile([P, H], U8, "res_scales")
+        out_rows = out_0.rearrange("(p t) c -> p t c", t=PACK)
+        out_words = out_1[0].rearrange("p c r -> p (c r)").bitcast(I32)
+        out_cuts = [slice(0, 256), slice(256, 384), slice(384, 512)]
+        for c in out_cuts:
+            entries = n3_sb[:, c.start // LANES : c.stop // LANES]
+            nc.vector.tensor_copy(gate[:, 0, c], window[0][:].indirect(entries))
+            for t in range(1, PACK):
+                nc.scalar.activation(gate[:, t, c], window[t][:].indirect(entries), ACT.Sigmoid)
+        for c in out_cuts:
+            for i in range(c.start // P, c.stop // P):
+                nc.vector.tensor_tensor(res[:, :, quarters[i]], h_ps[i][:], gate[:, :, quarters[i]], ALU.mult)
+            nc.sync.dma_start(out_rows[:, :, c], res[:, :, c])
+            packed = slice(c.start * PACK, c.stop * PACK)
+            nc.vector.tensor_copy(woven(res_bf[:, packed]), planar(res[:, :, c]))
+            nc.vector.quantize_mx(out=res_codes[:, c].bitcast(FP8X4), scales=res_scales[:, c], in_=res_bf[:, packed])
+            nc.sync.dma_start(out_words[:, c], res_codes[:, c])
+        for q in range(4):
+            queue = nc.sync if q % 2 == 0 else nc.scalar
+            queue.dma_start(
+                out_2[0, 4 * q : 4 * q + 4, :].bitcast(I32), res_scales[32 * q : 32 * q + 4, :].bitcast(I32)
+            )

@@ -1,6 +1,7 @@
 from contextlib import ExitStack
 
 import concourse.mybir as mybir
+from concourse.masks import make_identity
 
 K, T, S, N, H = 512, 2048, 512, 512, 512
 FLOPS = 2 * K * S * H + 2 * S * N * H
@@ -57,13 +58,14 @@ def tile_picked_tokkerngate_none_po_kernel(
             nc.sync.dma_start(
                 xs_all[32 * q : 32 * q + 4, :].bitcast(I32), x_scales[0, 4 * q : 4 * q + 4, :].bitcast(I32)
             )
-        nc.sync.dma_start(xw_all[:], x_words[0].rearrange("p c r -> p (c r)").bitcast(I32))
         wa_rows = wa.rearrange("(p j) c -> p j c", j=PACK)
-        for raw, c in zip(wa_raw, wa_cuts):
+        nc.sync.dma_start(wa_raw[0][:], wa_rows[:, :, wa_cuts[0]])
+        nc.sync.dma_start(xw_all[:], x_words[0].rearrange("p c r -> p (c r)").bitcast(I32))
+        for raw, c in zip(wa_raw[1:], wa_cuts[1:]):
             nc.sync.dma_start(raw[:], wa_rows[:, :, c])
+        nc.sync.dma_start(w1w_raw[:].bitcast(I32), w1_words[0].bitcast(I32))
         nc.sync.dma_start(n1_sb[:], n1)
         nc.sync.dma_start(n2_sb[:], n2)
-        nc.sync.dma_start(w1w_raw[:].bitcast(I32), w1_words[0].bitcast(I32))
         for q in range(4):
             nc.sync.dma_start(
                 w1s_raw[32 * q : 32 * q + 4, :].bitcast(I32), w1_scales[0, 4 * q : 4 * q + 4, :].bitcast(I32)
@@ -76,10 +78,10 @@ def tile_picked_tokkerngate_none_po_kernel(
         xw_dealt = tile([P, S], U32, "xw_dealt")
         nc.vector.tensor_copy(xs_picked[:], xs_all[:].indirect(offs_sb[:]))
         nc.vector.tensor_copy(
-            xw_dealt[:].rearrange("p (t m) -> p m t", t=PACK), xw_all[:].bitcast(U32).indirect(offs_sb[:])
+            xs_dealt[:].rearrange("p (t m) -> p t m", t=PACK), xs_picked[:].rearrange("p (m t) -> p t m", t=PACK)
         )
         nc.vector.tensor_copy(
-            xs_dealt[:].rearrange("p (t m) -> p t m", t=PACK), xs_picked[:].rearrange("p (m t) -> p t m", t=PACK)
+            xw_dealt[:].rearrange("p (t m) -> p m t", t=PACK), xw_all[:].bitcast(U32).indirect(offs_sb[:])
         )
 
         def woven(ap):
@@ -91,15 +93,16 @@ def tile_picked_tokkerngate_none_po_kernel(
         wa_bf = [tile([P, (c.stop - c.start) * PACK], BF16, f"wa_bf{c.start}") for c in wa_cuts]
         wa_codes = tile([P, H], U32, "wa_codes")
         wa_scales = tile([P, H], U8, "wa_scales")
-        y_ps = [ps.tile([P, H], F32, name=f"y_ps{t}") for t in range(PACK)]
+        y_ps = [ps.tile([P, H], F32, name=f"y_ps{t}", tag=f"bank{t}") for t in range(PACK)]
         for i, c in enumerate(wa_cuts):
             if i < len(wa_cuts) - 1:
                 nc.scalar.copy(woven(wa_bf[i][:]), planar(wa_raw[i][:]))
             else:
                 nc.vector.tensor_copy(woven(wa_bf[i][:]), planar(wa_raw[i][:]))
             nc.vector.quantize_mx(out=wa_codes[:, c].bitcast(FP8X4), scales=wa_scales[:, c], in_=wa_bf[i][:])
-            for t in range(PACK):
-                cols = slice(t * P, (t + 1) * P)
+        for t in range(PACK):
+            cols = slice(t * P, (t + 1) * P)
+            for c in wa_cuts:
                 nc.tensor.matmul_mx(
                     out=y_ps[t][:, c],
                     lhsT=xw_dealt[:, cols].bitcast(FP8X4),
@@ -110,13 +113,15 @@ def tile_picked_tokkerngate_none_po_kernel(
                     stop=True,
                 )
 
+        ident = tile([P, P], F32, "ident")
+        make_identity(nc, ident[:])
         w1w_dealt = tile([P, 2 * N], U8, "w1w_dealt")
         w1s_dealt = tile([P, N], U8, "w1s_dealt")
         nc.vector.tensor_copy(
             w1w_dealt[:].rearrange("p (t m b) -> p t m b", t=PACK, b=2),
             w1w_raw[:].rearrange("p (m t b) -> p t m b", t=PACK, b=2),
         )
-        nc.vector.tensor_copy(
+        nc.gpsimd.tensor_copy(
             w1s_dealt[:].rearrange("p (t m) -> p t m", t=PACK), w1s_raw[:].rearrange("p (m t) -> p t m", t=PACK)
         )
 
@@ -125,61 +130,71 @@ def tile_picked_tokkerngate_none_po_kernel(
         diff = [tile([P, 2, H], F32, f"diff{t}") for t in range(PACK)]
         sq = [tile([P, 2, H], F32, f"sq{t}") for t in range(PACK)]
         kern = [tile([P, 2, H], F32, f"kern{t}") for t in range(PACK)]
-        prod = [tile([P, 2, H], F32, f"prod{t}") for t in range(PACK)]
-        den = tile([P, PACK, H], F32, "den")
+        prod = tile([P, PACK, 2, H], F32, "prod")
         den_sq = tile([P, PACK, H], F32, "den_sq")
-        inv = tile([P, PACK, H], F32, "inv")
+        inv_t = [tile([P, PACK, HALF], F32, f"inv_t{h}") for h in range(2)]
         num = tile([P, PACK, H], F32, "num")
 
         for t in range(PACK):
             nc.scalar.copy(y_sb[t][:], y_ps[t][:])
+
+        def denominator(t):
+            den_ps = ps.tile([P, H], F32, name="den_ps", tag="den_ps", bufs=2)
+            for c in quarters:
+                for e in range(2):
+                    nc.tensor.matmul(
+                        den_ps[:, c], kern[t][:, e, c], ident[:], start=e == 0, stop=e == 1, is_transpose=True
+                    )
+            nc.scalar.activation(den_sq[:, t, :], den_ps[:], ACT.Square, bias=0.5)
+
         for t in range(PACK):
             for e, lst in enumerate((n1_sb, n2_sb)):
                 for h in range(2):
                     nc.vector.tensor_copy(near[t][:, e, halves[h]], y_sb[t][:].indirect(lst[:, list_halves[h]]))
-            for e in range(2):
-                nc.vector.tensor_tensor(diff[t][:, e, :], y_ps[t][:], near[t][:, e, :], ALU.subtract)
+            nc.gpsimd.tensor_tensor(diff[t][:, 0, :], y_sb[t][:], near[t][:, 0, :], ALU.subtract)
+            nc.vector.tensor_tensor(diff[t][:, 1, :], y_ps[t][:], near[t][:, 1, :], ALU.subtract)
             for e in range(2):
                 nc.scalar.activation(sq[t][:, e, :], diff[t][:, e, :], ACT.Square)
             for e in range(2):
                 nc.scalar.activation(kern[t][:, e, :], sq[t][:, e, :], ACT.Exp, scale=-0.5)
-
-        def denominator(t):
-            nc.vector.scalar_tensor_tensor(den[:, t, :], kern[t][:, 0, :], 0.5, kern[t][:, 1, :], ALU.add, ALU.add)
-            nc.scalar.activation(den_sq[:, t, :], den[:, t, :], ACT.Square)
+            if t > 0:
+                denominator(t - 1)
 
         def products(t):
             nc.vector.scalar_tensor_tensor(
-                prod[t][:], kern[t][:], gt_sb[:, t : t + 1], near[t][:], ALU.mult, ALU.mult
+                prod[:, t, :, :], kern[t][:], gt_sb[:, t : t + 1], near[t][:], ALU.mult, ALU.mult
             )
 
-        def numerator(t):
-            nc.vector.tensor_tensor(num[:, t, :], prod[t][:, 0, :], prod[t][:, 1, :], ALU.add)
+        def numerator(c):
+            nc.vector.tensor_tensor(num[:, :, c], prod[:, :, 0, c], prod[:, :, 1, c], ALU.add)
 
-        for t in range(PACK - 1):
-            denominator(t)
-        products(0)
         denominator(PACK - 1)
-        for t in range(1, PACK):
+        inv_ps = []
+        for h in range(2):
+            nc.scalar.activation(inv_t[h][:], den_sq[:, :, halves[h]], ACT.Abs_reciprocal_sqrt)
+            for i in (2 * h, 2 * h + 1):
+                inv_ps.append(ps.tile([P, PACK, P], F32, name=f"inv_ps{i}", tag=f"bank{i}"))
+                for t in range(PACK):
+                    nc.tensor.transpose(inv_ps[i][:, t, :], inv_t[h][:, t, quarters[i % 2]], ident[:])
+        for t in range(PACK):
             products(t)
-            numerator(t - 1)
-        for c in quarters:
-            nc.scalar.activation(inv[:, :, c], den_sq[:, :, c], ACT.Abs_reciprocal_sqrt)
-        numerator(PACK - 1)
+        for c in halves:
+            numerator(c)
 
         z_bf = [tile([P, P * PACK], BF16, f"z_bf{i}") for i in range(4)]
         z_codes = tile([P, H], U32, "z_codes")
         z_scales = tile([P, H], U8, "z_scales")
-        h_ps = [ps.tile([P, PACK, P], F32, name=f"h_ps{i}") for i in range(4)]
+        h_ps = []
         window = [tile([P, H], F32, f"window{t}") for t in range(PACK)]
 
         def divide(i):
             c = quarters[i]
-            nc.vector.tensor_tensor(woven(z_bf[i][:]), planar(num[:, :, c]), planar(inv[:, :, c]), ALU.mult)
+            nc.vector.tensor_tensor(woven(z_bf[i][:]), planar(inv_ps[i][:]), planar(num[:, :, c]), ALU.mult)
 
         def second_product(i):
             c = quarters[i]
             nc.vector.quantize_mx(out=z_codes[:, c].bitcast(FP8X4), scales=z_scales[:, c], in_=z_bf[i][:])
+            h_ps.append(ps.tile([P, PACK, P], F32, name=f"h_ps{i}", tag=f"bank{i}"))
             for t in range(PACK):
                 nc.tensor.matmul_mx(
                     out=h_ps[i][:, t, :],
@@ -207,20 +222,47 @@ def tile_picked_tokkerngate_none_po_kernel(
         res_scales = tile([P, H], U8, "res_scales")
         out_rows = out_0.rearrange("(p t) c -> p t c", t=PACK)
         out_words = out_1[0].rearrange("p c r -> p (c r)").bitcast(I32)
-        out_cuts = [slice(0, 256), slice(256, 384), slice(384, 512)]
-        for c in out_cuts:
-            entries = n3_sb[:, c.start // LANES : c.stop // LANES]
-            nc.vector.tensor_copy(gate[:, 0, c], window[0][:].indirect(entries))
-            for t in range(1, PACK):
-                nc.scalar.activation(gate[:, t, c], window[t][:].indirect(entries), ACT.Sigmoid)
-        for c in out_cuts:
-            for i in range(c.start // P, c.stop // P):
-                nc.vector.tensor_tensor(res[:, :, quarters[i]], h_ps[i][:], gate[:, :, quarters[i]], ALU.mult)
-            nc.sync.dma_start(out_rows[:, :, c], res[:, :, c])
-            packed = slice(c.start * PACK, c.stop * PACK)
-            nc.vector.tensor_copy(woven(res_bf[:, packed]), planar(res[:, :, c]))
-            nc.vector.quantize_mx(out=res_codes[:, c].bitcast(FP8X4), scales=res_scales[:, c], in_=res_bf[:, packed])
+
+        def entries(c):
+            return n3_sb[:, c.start // LANES : c.stop // LANES]
+
+        def packed(c):
+            return res_bf[:, c.start * PACK : c.stop * PACK]
+
+        def fetch_first(i):
+            nc.vector.tensor_copy(gate[:, 0, quarters[i]], window[0][:].indirect(entries(quarters[i])))
+
+        def gated(i):
+            nc.vector.tensor_tensor(res[:, :, quarters[i]], h_ps[i][:], gate[:, :, quarters[i]], ALU.mult)
+
+        def weave(i):
+            nc.vector.tensor_copy(woven(packed(quarters[i])), planar(res[:, :, quarters[i]]))
+
+        def planes(c):
+            nc.vector.quantize_mx(out=res_codes[:, c].bitcast(FP8X4), scales=res_scales[:, c], in_=packed(c))
             nc.sync.dma_start(out_words[:, c], res_codes[:, c])
+
+        for c in quarters:
+            for t in range(1, PACK):
+                nc.scalar.activation(gate[:, t, c], window[t][:].indirect(entries(c)), ACT.Sigmoid)
+        fetch_first(0)
+        fetch_first(1)
+        fetch_first(2)
+        fetch_first(3)
+        gated(0)
+        gated(1)
+        nc.sync.dma_start(out_rows[:, :, halves[0]], res[:, :, halves[0]])
+        weave(0)
+        gated(2)
+        nc.sync.dma_start(out_rows[:, :, quarters[2]], res[:, :, quarters[2]])
+        weave(1)
+        nc.scalar.copy(woven(packed(quarters[2])), planar(res[:, :, quarters[2]]))
+        gated(3)
+        nc.sync.dma_start(out_rows[:, :, quarters[3]], res[:, :, quarters[3]])
+        planes(halves[0])
+        weave(3)
+        planes(quarters[2])
+        planes(quarters[3])
         for q in range(4):
             queue = nc.sync if q % 2 == 0 else nc.scalar
             queue.dma_start(

@@ -35,8 +35,8 @@ def tile_picked_tokkerngate_none_po_kernel(
         sb = ctx.enter_context(tc.tile_pool(name="sb", bufs=1))
         ps = ctx.enter_context(tc.psum_pool(name="ps", bufs=1))
 
-        def tile(shape, dtype, name):
-            return sb.tile(shape, dtype, name=name, align_bytes=64)
+        def tile(shape, dtype, name, tag=""):
+            return sb.tile(shape, dtype, name=name, tag=tag or name, align_bytes=64)
 
         offs_sb = tile([P, S // LANES], U16, "offs_sb")
         n1_sb = tile([P, H // LANES], U16, "n1_sb")
@@ -63,9 +63,9 @@ def tile_picked_tokkerngate_none_po_kernel(
         nc.sync.dma_start(xw_all[:], x_words[0].rearrange("p c r -> p (c r)").bitcast(I32))
         for raw, c in zip(wa_raw[1:], wa_cuts[1:]):
             nc.sync.dma_start(raw[:], wa_rows[:, :, c])
-        nc.sync.dma_start(w1w_raw[:].bitcast(I32), w1_words[0].bitcast(I32))
         nc.sync.dma_start(n1_sb[:], n1)
         nc.sync.dma_start(n2_sb[:], n2)
+        nc.sync.dma_start(w1w_raw[:].bitcast(I32), w1_words[0].bitcast(I32))
         for q in range(4):
             nc.sync.dma_start(
                 w1s_raw[32 * q : 32 * q + 4, :].bitcast(I32), w1_scales[0, 4 * q : 4 * q + 4, :].bitcast(I32)
@@ -94,6 +94,7 @@ def tile_picked_tokkerngate_none_po_kernel(
         wa_codes = tile([P, H], U32, "wa_codes")
         wa_scales = tile([P, H], U8, "wa_scales")
         y_ps = [ps.tile([P, H], F32, name=f"y_ps{t}", tag=f"bank{t}") for t in range(PACK)]
+        y_early = ps.tile([P, HALF], F32, name="y_early", tag="spare")
         for i, c in enumerate(wa_cuts):
             if i < len(wa_cuts) - 1:
                 nc.scalar.copy(woven(wa_bf[i][:]), planar(wa_raw[i][:]))
@@ -104,7 +105,7 @@ def tile_picked_tokkerngate_none_po_kernel(
             cols = slice(t * P, (t + 1) * P)
             for c in wa_cuts:
                 nc.tensor.matmul_mx(
-                    out=y_ps[t][:, c],
+                    out=y_early[:] if t == 0 and c == halves[0] else y_ps[t][:, c],
                     lhsT=xw_dealt[:, cols].bitcast(FP8X4),
                     lhsT_scale=xs_dealt[:, cols],
                     rhs=wa_codes[:, c].bitcast(FP8X4),
@@ -115,77 +116,112 @@ def tile_picked_tokkerngate_none_po_kernel(
 
         ident = tile([P, P], F32, "ident")
         make_identity(nc, ident[:])
-        w1w_dealt = tile([P, 2 * N], U8, "w1w_dealt")
-        w1s_dealt = tile([P, N], U8, "w1s_dealt")
-        nc.vector.tensor_copy(
+        w1w_dealt = tile([P, 2 * N], U8, "w1w_dealt", tag=f"wa_bf{wa_cuts[-1].start}")
+        nc.gpsimd.tensor_copy(
             w1w_dealt[:].rearrange("p (t m b) -> p t m b", t=PACK, b=2),
             w1w_raw[:].rearrange("p (m t b) -> p t m b", t=PACK, b=2),
-        )
-        nc.gpsimd.tensor_copy(
-            w1s_dealt[:].rearrange("p (t m) -> p t m", t=PACK), w1s_raw[:].rearrange("p (m t) -> p t m", t=PACK)
         )
 
         y_sb = [tile([P, H], F32, f"y_sb{t}") for t in range(PACK)]
         near = [tile([P, 2, H], F32, f"near{t}") for t in range(PACK)]
-        diff = [tile([P, 2, H], F32, f"diff{t}") for t in range(PACK)]
+        diff_all = tile([P, PACK + 1, 2, H], F32, "diff_all")
+        diff = [diff_all[:, t, :, :] for t in range(PACK)]
         sq = [tile([P, 2, H], F32, f"sq{t}") for t in range(PACK)]
         kern = [tile([P, 2, H], F32, f"kern{t}") for t in range(PACK)]
         prod = tile([P, PACK, 2, H], F32, "prod")
-        den_sq = tile([P, PACK, H], F32, "den_sq")
-        inv_t = [tile([P, PACK, HALF], F32, f"inv_t{h}") for h in range(2)]
+        den_sq = diff_all[:, 1:, 1, :]
         num = tile([P, PACK, H], F32, "num")
 
-        for t in range(PACK):
+        nc.scalar.copy(y_sb[0][:, halves[0]], y_early[:])
+        nc.scalar.copy(y_sb[0][:, halves[1]], y_ps[0][:, halves[1]])
+        for t in range(1, PACK):
             nc.scalar.copy(y_sb[t][:], y_ps[t][:])
 
-        def denominator(t):
+        def kernel_sum(t):
             den_ps = ps.tile([P, H], F32, name="den_ps", tag="den_ps", bufs=2)
             for c in quarters:
                 for e in range(2):
                     nc.tensor.matmul(
                         den_ps[:, c], kern[t][:, e, c], ident[:], start=e == 0, stop=e == 1, is_transpose=True
                     )
-            nc.scalar.activation(den_sq[:, t, :], den_ps[:], ACT.Square, bias=0.5)
+            return den_ps
 
+        def square(t, den_ps, c):
+            nc.scalar.activation(den_sq[:, t, c], den_ps[:, c], ACT.Square, bias=0.5)
+
+        last = PACK - 1
         for t in range(PACK):
             for e, lst in enumerate((n1_sb, n2_sb)):
                 for h in range(2):
                     nc.vector.tensor_copy(near[t][:, e, halves[h]], y_sb[t][:].indirect(lst[:, list_halves[h]]))
-            nc.gpsimd.tensor_tensor(diff[t][:, 0, :], y_sb[t][:], near[t][:, 0, :], ALU.subtract)
-            nc.vector.tensor_tensor(diff[t][:, 1, :], y_ps[t][:], near[t][:, 1, :], ALU.subtract)
             for e in range(2):
-                nc.scalar.activation(sq[t][:, e, :], diff[t][:, e, :], ACT.Square)
-            for e in range(2):
-                nc.scalar.activation(kern[t][:, e, :], sq[t][:, e, :], ACT.Exp, scale=-0.5)
+                if t < last:
+                    nc.gpsimd.tensor_tensor(diff[t][:, e, :], y_sb[t][:], near[t][:, e, :], ALU.subtract)
+                else:
+                    nc.vector.tensor_tensor(diff[t][:, e, :], y_ps[t][:], near[t][:, e, :], ALU.subtract)
+                for c in reversed(halves):
+                    nc.scalar.activation(sq[t][:, e, c], diff[t][:, e, c], ACT.Square)
+                for c in reversed(halves):
+                    nc.scalar.activation(kern[t][:, e, c], sq[t][:, e, c], ACT.Exp, scale=-0.5)
             if t > 0:
-                denominator(t - 1)
+                square(t - 1, kernel_sum(t - 1), slice(0, H))
 
-        def products(t):
+        w1s_dealt = tile([P, N], U8, "w1s_dealt", tag=f"y_sb{last - 1}")
+        nc.gpsimd.tensor_copy(
+            w1s_dealt[:].rearrange("p (t m) -> p t m", t=PACK), w1s_raw[:].rearrange("p (m t) -> p t m", t=PACK)
+        )
+
+        def products(t, c):
             nc.vector.scalar_tensor_tensor(
-                prod[:, t, :, :], kern[t][:], gt_sb[:, t : t + 1], near[t][:], ALU.mult, ALU.mult
+                prod[:, t, :, c], kern[t][:, :, c], gt_sb[:, t : t + 1], near[t][:, :, c], ALU.mult, ALU.mult
             )
 
-        def numerator(c):
-            nc.vector.tensor_tensor(num[:, :, c], prod[:, :, 0, c], prod[:, :, 1, c], ALU.add)
+        def numerator(rows, c):
+            nc.vector.tensor_tensor(num[:, rows, c], prod[:, rows, 0, c], prod[:, rows, 1, c], ALU.add)
 
-        denominator(PACK - 1)
+        inv_t = [sq[last][:].rearrange("p e (u c) -> p (e u) c", u=2), den_sq[:, :, halves[0]]]
+        early, late, every = slice(0, last), slice(last, PACK), slice(0, PACK)
+
+        def invert(rows, c):
+            h = c.start // HALF
+            inner = slice(c.start - h * HALF, c.stop - h * HALF)
+            nc.scalar.activation(inv_t[h][:, rows, inner], den_sq[:, rows, c], ACT.Abs_reciprocal_sqrt)
+
         inv_ps = []
-        for h in range(2):
-            nc.scalar.activation(inv_t[h][:], den_sq[:, :, halves[h]], ACT.Abs_reciprocal_sqrt)
-            for i in (2 * h, 2 * h + 1):
-                inv_ps.append(ps.tile([P, PACK, P], F32, name=f"inv_ps{i}", tag=f"bank{i}"))
-                for t in range(PACK):
-                    nc.tensor.transpose(inv_ps[i][:, t, :], inv_t[h][:, t, quarters[i % 2]], ident[:])
-        for t in range(PACK):
-            products(t)
+
+        def turn_back(i):
+            inv_ps.append(ps.tile([P, PACK, P], F32, name=f"inv_ps{i}", tag=f"bank{i}"))
+            for t in range(PACK):
+                nc.tensor.transpose(inv_ps[i][:, t, :], inv_t[i // 2][:, t, quarters[i % 2]], ident[:])
+
+        den_last = kernel_sum(last)
+        invert(early, quarters[0])
+        square(last, den_last, halves[0])
+        invert(early, quarters[1])
+        invert(late, halves[0])
+        turn_back(0)
+        turn_back(1)
+        square(last, den_last, halves[1])
+        invert(early, quarters[2])
+        invert(late, quarters[2])
+        turn_back(2)
+        invert(every, quarters[3])
+        turn_back(3)
+
+        for t in range(last):
+            products(t, slice(0, H))
+        numerator(slice(0, last - 1), slice(0, H))
         for c in halves:
-            numerator(c)
+            products(last, c)
+        numerator(slice(last - 1, last), slice(0, H))
+        numerator(late, slice(0, H))
 
         z_bf = [tile([P, P * PACK], BF16, f"z_bf{i}") for i in range(4)]
         z_codes = tile([P, H], U32, "z_codes")
         z_scales = tile([P, H], U8, "z_scales")
         h_ps = []
-        window = [tile([P, H], F32, f"window{t}") for t in range(PACK)]
+        h_late = ps.tile([P, PACK, P], F32, name="h_late", tag="spare")
+        window = {t: tile([P, H], F32, f"window{t}") for t in (0, 1, 3)}
 
         def divide(i):
             c = quarters[i]
@@ -197,7 +233,7 @@ def tile_picked_tokkerngate_none_po_kernel(
             h_ps.append(ps.tile([P, PACK, P], F32, name=f"h_ps{i}", tag=f"bank{i}"))
             for t in range(PACK):
                 nc.tensor.matmul_mx(
-                    out=h_ps[i][:, t, :],
+                    out=h_late[:, t, :] if i == 3 and t >= 1 else h_ps[i][:, t, :],
                     lhsT=w1w_dealt[:, 2 * t * P : 2 * (t + 1) * P].bitcast(FP4X4),
                     lhsT_scale=w1s_dealt[:, t * P : (t + 1) * P],
                     rhs=z_codes[:, c].bitcast(FP8X4),
@@ -205,15 +241,25 @@ def tile_picked_tokkerngate_none_po_kernel(
                     start=True,
                     stop=True,
                 )
+            if i == 2:
+                for t in (1, 3):
+                    nc.vector.tensor_copy(window[t][:, c], h_ps[i][:, t, :])
             nc.scalar.activation(window[0][:, c], h_ps[i][:, 0, :], ACT.Sigmoid)
-            for t in range(1, PACK):
-                nc.scalar.copy(window[t][:, c], h_ps[i][:, t, :])
+            if i < 2:
+                for t in (1, 3):
+                    nc.scalar.copy(window[t][:, c], h_ps[i][:, t, :])
+
+        def h_rows(i, rows):
+            return (h_late if i == 3 and rows.start >= 1 else h_ps[i])[:, rows, :]
 
         divide(0)
         for i in range(1, 4):
             divide(i)
             second_product(i - 1)
         second_product(3)
+        window.setdefault(2, tile([P, H], F32, "window2", tag="num"))
+        for t, i in [(2, 0), (2, 1), (2, 2), (3, 3), (2, 3), (1, 3)]:
+            nc.vector.tensor_copy(window[t][:, quarters[i]].unsqueeze(1), h_rows(i, slice(t, t + 1)))
 
         gate = tile([P, PACK, H], F32, "gate")
         res = tile([P, PACK, H], F32, "res")
@@ -232,8 +278,8 @@ def tile_picked_tokkerngate_none_po_kernel(
         def fetch_first(i):
             nc.vector.tensor_copy(gate[:, 0, quarters[i]], window[0][:].indirect(entries(quarters[i])))
 
-        def gated(i):
-            nc.vector.tensor_tensor(res[:, :, quarters[i]], h_ps[i][:], gate[:, :, quarters[i]], ALU.mult)
+        def gated(i, rows):
+            nc.vector.tensor_tensor(res[:, rows, quarters[i]], h_rows(i, rows), gate[:, rows, quarters[i]], ALU.mult)
 
         def weave(i):
             nc.vector.tensor_copy(woven(packed(quarters[i])), planar(res[:, :, quarters[i]]))
@@ -245,24 +291,27 @@ def tile_picked_tokkerngate_none_po_kernel(
         for c in quarters:
             for t in range(1, PACK):
                 nc.scalar.activation(gate[:, t, c], window[t][:].indirect(entries(c)), ACT.Sigmoid)
-        fetch_first(0)
-        fetch_first(1)
-        fetch_first(2)
-        fetch_first(3)
-        gated(0)
-        gated(1)
-        nc.sync.dma_start(out_rows[:, :, halves[0]], res[:, :, halves[0]])
-        weave(0)
-        gated(2)
-        nc.sync.dma_start(out_rows[:, :, quarters[2]], res[:, :, quarters[2]])
-        weave(1)
-        nc.scalar.copy(woven(packed(quarters[2])), planar(res[:, :, quarters[2]]))
-        gated(3)
-        nc.sync.dma_start(out_rows[:, :, quarters[3]], res[:, :, quarters[3]])
+        for i in range(4):
+            fetch_first(i)
+        for i in range(3):
+            gated(i, slice(0, PACK))
+            if i < 2:
+                nc.gpsimd.tensor_copy(
+                    packed(quarters[i]).rearrange("p (c t) -> p c t", t=PACK),
+                    res[:, :, quarters[i]].rearrange("p t c -> p c t"),
+                )
+            else:
+                nc.scalar.copy(woven(packed(quarters[i])), planar(res[:, :, quarters[i]]))
+            if i > 0:
+                c = halves[0] if i == 1 else quarters[i]
+                nc.sync.dma_start(out_rows[:, :, c], res[:, :, c])
+        gated(3, slice(0, 1))
+        gated(3, slice(1, last))
         planes(halves[0])
+        gated(3, late)
+        nc.sync.dma_start(out_rows[:, :, quarters[3]], res[:, :, quarters[3]])
         weave(3)
-        planes(quarters[2])
-        planes(quarters[3])
+        planes(halves[1])
         for q in range(4):
             queue = nc.sync if q % 2 == 0 else nc.scalar
             queue.dma_start(

@@ -19,8 +19,12 @@ ALU = mybir.AluOpType
 
 P = 128
 PACK = 4
+LAST = PACK - 1
 HALF = H // 2
+PARTS = H // P
 LANES = 16
+QUADS = 4
+RUN = 4
 
 
 def tile_picked_tokkerngate_none_po_kernel(
@@ -28,8 +32,21 @@ def tile_picked_tokkerngate_none_po_kernel(
 ):
     nc = tc.nc
     halves = [slice(h * HALF, (h + 1) * HALF) for h in range(2)]
-    quarters = [slice(i * P, (i + 1) * P) for i in range(4)]
-    list_halves = [slice(h * HALF // LANES, (h + 1) * HALF // LANES) for h in range(2)]
+    quarters = [slice(i * P, (i + 1) * P) for i in range(PARTS)]
+    all_cols = slice(0, H)
+    early, late, every = slice(0, LAST), slice(LAST, PACK), slice(0, PACK)
+
+    def live_rows(plane, q):
+        return plane[32 * q : 32 * q + 4, :].bitcast(I32)
+
+    def hbm_rows(scales, q):
+        return scales[0, 4 * q : 4 * q + 4, :].bitcast(I32)
+
+    def woven(ap):
+        return ap.rearrange("p (c i t) -> p c t i", i=RUN, t=PACK)
+
+    def planar(ap):
+        return ap.rearrange("p t (c i) -> p c t i", i=RUN)
 
     with ExitStack() as ctx:
         sb = ctx.enter_context(tc.tile_pool(name="sb", bufs=1))
@@ -46,18 +63,20 @@ def tile_picked_tokkerngate_none_po_kernel(
         xs_all = tile([P, T], U8, "xs_all")
         w1w_raw = tile([P, 2 * N], U8, "w1w_raw")
         w1s_raw = tile([P, N], U8, "w1s_raw")
-        wa_cuts = [slice(0, 256), slice(256, 384), slice(384, 512)]
+        wa_cuts = [halves[0], quarters[2], quarters[3]]
         wa_raw = [tile([P, PACK, c.stop - c.start], F32, f"wa_raw{c.start}") for c in wa_cuts]
         gt_sb = tile([P, PACK], F32, "gt_sb")
 
         nc.vector.memset(xs_all[:].bitcast(I32), 0)
         nc.vector.memset(w1s_raw[:].bitcast(I32), 0)
+        y_wide = [tile([P, 2 * H], F32, f"y_wide{t}") for t in range(PACK)]
+        y_sb = [wide[:, :H] for wide in y_wide]
+        for wide in y_wide:
+            nc.vector.memset(wide[:, H:], 0.0)
 
         nc.sync.dma_start(offs_sb[:], offs)
-        for q in range(4):
-            nc.sync.dma_start(
-                xs_all[32 * q : 32 * q + 4, :].bitcast(I32), x_scales[0, 4 * q : 4 * q + 4, :].bitcast(I32)
-            )
+        for q in range(QUADS):
+            nc.sync.dma_start(live_rows(xs_all, q), hbm_rows(x_scales, q))
         wa_rows = wa.rearrange("(p j) c -> p j c", j=PACK)
         nc.sync.dma_start(wa_raw[0][:], wa_rows[:, :, wa_cuts[0]])
         nc.sync.dma_start(xw_all[:], x_words[0].rearrange("p c r -> p (c r)").bitcast(I32))
@@ -66,10 +85,8 @@ def tile_picked_tokkerngate_none_po_kernel(
         nc.sync.dma_start(n1_sb[:], n1)
         nc.sync.dma_start(n2_sb[:], n2)
         nc.sync.dma_start(w1w_raw[:].bitcast(I32), w1_words[0].bitcast(I32))
-        for q in range(4):
-            nc.sync.dma_start(
-                w1s_raw[32 * q : 32 * q + 4, :].bitcast(I32), w1_scales[0, 4 * q : 4 * q + 4, :].bitcast(I32)
-            )
+        for q in range(QUADS):
+            nc.sync.dma_start(live_rows(w1s_raw, q), hbm_rows(w1_scales, q))
         nc.sync.dma_start(gt_sb[:], gt.rearrange("(p t) o -> p (t o)", t=PACK))
         nc.sync.dma_start(n3_sb[:], n3)
 
@@ -84,12 +101,6 @@ def tile_picked_tokkerngate_none_po_kernel(
             xw_dealt[:].rearrange("p (t m) -> p m t", t=PACK), xw_all[:].bitcast(U32).indirect(offs_sb[:])
         )
 
-        def woven(ap):
-            return ap.rearrange("p (c i t) -> p c t i", i=4, t=PACK)
-
-        def planar(ap):
-            return ap.rearrange("p t (c i) -> p c t i", i=4)
-
         wa_bf = [tile([P, (c.stop - c.start) * PACK], BF16, f"wa_bf{c.start}") for c in wa_cuts]
         wa_codes = tile([P, H], U32, "wa_codes")
         wa_scales = tile([P, H], U8, "wa_scales")
@@ -102,12 +113,12 @@ def tile_picked_tokkerngate_none_po_kernel(
                 nc.vector.tensor_copy(woven(wa_bf[i][:]), planar(wa_raw[i][:]))
             nc.vector.quantize_mx(out=wa_codes[:, c].bitcast(FP8X4), scales=wa_scales[:, c], in_=wa_bf[i][:])
         for t in range(PACK):
-            cols = slice(t * P, (t + 1) * P)
+            tokens = slice(t * P, (t + 1) * P)
             for c in wa_cuts:
                 nc.tensor.matmul_mx(
                     out=y_early[:] if t == 0 and c == halves[0] else y_ps[t][:, c],
-                    lhsT=xw_dealt[:, cols].bitcast(FP8X4),
-                    lhsT_scale=xs_dealt[:, cols],
+                    lhsT=xw_dealt[:, tokens].bitcast(FP8X4),
+                    lhsT_scale=xs_dealt[:, tokens],
                     rhs=wa_codes[:, c].bitcast(FP8X4),
                     rhs_scale=wa_scales[:, c],
                     start=True,
@@ -122,7 +133,6 @@ def tile_picked_tokkerngate_none_po_kernel(
             w1w_raw[:].rearrange("p (m t b) -> p t m b", t=PACK, b=2),
         )
 
-        y_sb = [tile([P, H], F32, f"y_sb{t}") for t in range(PACK)]
         near = [tile([P, 2, H], F32, f"near{t}") for t in range(PACK)]
         diff_all = tile([P, PACK + 1, 2, H], F32, "diff_all")
         diff = [diff_all[:, t, :, :] for t in range(PACK)]
@@ -135,7 +145,7 @@ def tile_picked_tokkerngate_none_po_kernel(
         nc.scalar.copy(y_sb[0][:, halves[0]], y_early[:])
         nc.scalar.copy(y_sb[0][:, halves[1]], y_ps[0][:, halves[1]])
         for t in range(1, PACK):
-            nc.scalar.copy(y_sb[t][:], y_ps[t][:])
+            nc.scalar.copy(y_sb[t], y_ps[t][:])
 
         def kernel_sum(t):
             den_ps = ps.tile([P, H], F32, name="den_ps", tag="den_ps", bufs=2)
@@ -149,14 +159,16 @@ def tile_picked_tokkerngate_none_po_kernel(
         def square(t, den_ps, c):
             nc.scalar.activation(den_sq[:, t, c], den_ps[:, c], ACT.Square, bias=0.5)
 
-        last = PACK - 1
         for t in range(PACK):
             for e, lst in enumerate((n1_sb, n2_sb)):
-                for h in range(2):
-                    nc.vector.tensor_copy(near[t][:, e, halves[h]], y_sb[t][:].indirect(lst[:, list_halves[h]]))
+                nc.vector.tensor_copy(near[t][:, e, :], y_wide[t][:].indirect(lst[:]))
             for e in range(2):
-                if t < last:
-                    nc.gpsimd.tensor_tensor(diff[t][:, e, :], y_sb[t][:], near[t][:, e, :], ALU.subtract)
+                if t < LAST:
+                    nc.gpsimd.tensor_tensor(diff[t][:, e, :], y_sb[t], near[t][:, e, :], ALU.subtract)
+                elif e == 0:
+                    low, high = halves
+                    nc.vector.tensor_tensor(diff[t][:, e, high], y_ps[t][:, high], near[t][:, e, high], ALU.subtract)
+                    nc.gpsimd.tensor_tensor(diff[t][:, e, low], y_sb[t][:, low], near[t][:, e, low], ALU.subtract)
                 else:
                     nc.vector.tensor_tensor(diff[t][:, e, :], y_ps[t][:], near[t][:, e, :], ALU.subtract)
                 for c in reversed(halves):
@@ -164,23 +176,9 @@ def tile_picked_tokkerngate_none_po_kernel(
                 for c in reversed(halves):
                     nc.scalar.activation(kern[t][:, e, c], sq[t][:, e, c], ACT.Exp, scale=-0.5)
             if t > 0:
-                square(t - 1, kernel_sum(t - 1), slice(0, H))
+                square(t - 1, kernel_sum(t - 1), all_cols)
 
-        w1s_dealt = tile([P, N], U8, "w1s_dealt", tag=f"y_sb{last - 1}")
-        nc.gpsimd.tensor_copy(
-            w1s_dealt[:].rearrange("p (t m) -> p t m", t=PACK), w1s_raw[:].rearrange("p (m t) -> p t m", t=PACK)
-        )
-
-        def products(t, c):
-            nc.vector.scalar_tensor_tensor(
-                prod[:, t, :, c], kern[t][:, :, c], gt_sb[:, t : t + 1], near[t][:, :, c], ALU.mult, ALU.mult
-            )
-
-        def numerator(rows, c):
-            nc.vector.tensor_tensor(num[:, rows, c], prod[:, rows, 0, c], prod[:, rows, 1, c], ALU.add)
-
-        inv_t = [sq[last][:].rearrange("p e (u c) -> p (e u) c", u=2), den_sq[:, :, halves[0]]]
-        early, late, every = slice(0, last), slice(last, PACK), slice(0, PACK)
+        inv_t = [sq[LAST][:].rearrange("p e (u c) -> p (e u) c", u=2), den_sq[:, :, halves[0]]]
 
         def invert(rows, c):
             h = c.start // HALF
@@ -194,31 +192,45 @@ def tile_picked_tokkerngate_none_po_kernel(
             for t in range(PACK):
                 nc.tensor.transpose(inv_ps[i][:, t, :], inv_t[i // 2][:, t, quarters[i % 2]], ident[:])
 
-        den_last = kernel_sum(last)
+        den_last = kernel_sum(LAST)
         invert(early, quarters[0])
-        square(last, den_last, halves[0])
+        square(LAST, den_last, halves[0])
         invert(early, quarters[1])
         invert(late, halves[0])
         turn_back(0)
         turn_back(1)
-        square(last, den_last, halves[1])
+        square(LAST, den_last, halves[1])
         invert(early, quarters[2])
         invert(late, quarters[2])
         turn_back(2)
         invert(every, quarters[3])
         turn_back(3)
 
-        for t in range(last):
-            products(t, slice(0, H))
-        numerator(slice(0, last - 1), slice(0, H))
-        for c in halves:
-            products(last, c)
-        numerator(slice(last - 1, last), slice(0, H))
-        numerator(late, slice(0, H))
+        def products(t, c):
+            nc.vector.scalar_tensor_tensor(
+                prod[:, t, :, c], kern[t][:, :, c], gt_sb[:, t : t + 1], near[t][:, :, c], ALU.mult, ALU.mult
+            )
 
-        z_bf = [tile([P, P * PACK], BF16, f"z_bf{i}") for i in range(4)]
+        def numerator(rows):
+            nc.vector.tensor_tensor(num[:, rows, :], prod[:, rows, 0, :], prod[:, rows, 1, :], ALU.add)
+
+        for t in range(LAST):
+            products(t, all_cols)
+        numerator(slice(0, LAST - 1))
+        for c in halves:
+            products(LAST, c)
+        numerator(slice(LAST - 1, LAST))
+        numerator(late)
+
+        w1s_dealt = tile([P, N], U8, "w1s_dealt", tag="prod")
+        nc.gpsimd.tensor_copy(
+            w1s_dealt[:].rearrange("p (t m) -> p t m", t=PACK), w1s_raw[:].rearrange("p (m t) -> p t m", t=PACK)
+        )
+
+        z_bf = [tile([P, P * PACK], BF16, f"z_bf{i}") for i in range(PARTS)]
         z_codes = tile([P, H], U32, "z_codes")
         z_scales = tile([P, H], U8, "z_scales")
+        final = PARTS - 1
         h_ps = []
         h_late = ps.tile([P, PACK, P], F32, name="h_late", tag="spare")
         window = {t: tile([P, H], F32, f"window{t}") for t in (0, 1, 3)}
@@ -227,13 +239,16 @@ def tile_picked_tokkerngate_none_po_kernel(
             c = quarters[i]
             nc.vector.tensor_tensor(woven(z_bf[i][:]), planar(inv_ps[i][:]), planar(num[:, :, c]), ALU.mult)
 
+        def h_rows(i, rows):
+            return (h_late if i == final and rows.start >= 1 else h_ps[i])[:, rows, :]
+
         def second_product(i):
             c = quarters[i]
             nc.vector.quantize_mx(out=z_codes[:, c].bitcast(FP8X4), scales=z_scales[:, c], in_=z_bf[i][:])
             h_ps.append(ps.tile([P, PACK, P], F32, name=f"h_ps{i}", tag=f"bank{i}"))
             for t in range(PACK):
                 nc.tensor.matmul_mx(
-                    out=h_late[:, t, :] if i == 3 and t >= 1 else h_ps[i][:, t, :],
+                    out=h_late[:, t, :] if i == final and t >= 1 else h_ps[i][:, t, :],
                     lhsT=w1w_dealt[:, 2 * t * P : 2 * (t + 1) * P].bitcast(FP4X4),
                     lhsT_scale=w1s_dealt[:, t * P : (t + 1) * P],
                     rhs=z_codes[:, c].bitcast(FP8X4),
@@ -241,24 +256,21 @@ def tile_picked_tokkerngate_none_po_kernel(
                     start=True,
                     stop=True,
                 )
-            if i == 2:
+            if i == final - 1:
                 for t in (1, 3):
                     nc.vector.tensor_copy(window[t][:, c], h_ps[i][:, t, :])
             nc.scalar.activation(window[0][:, c], h_ps[i][:, 0, :], ACT.Sigmoid)
-            if i < 2:
+            if i < final - 1:
                 for t in (1, 3):
                     nc.scalar.copy(window[t][:, c], h_ps[i][:, t, :])
 
-        def h_rows(i, rows):
-            return (h_late if i == 3 and rows.start >= 1 else h_ps[i])[:, rows, :]
-
         divide(0)
-        for i in range(1, 4):
+        for i in range(1, PARTS):
             divide(i)
             second_product(i - 1)
-        second_product(3)
+        second_product(final)
         window.setdefault(2, tile([P, H], F32, "window2", tag="num"))
-        for t, i in [(2, 0), (2, 1), (2, 2), (3, 3), (2, 3), (1, 3)]:
+        for t, i in [(2, i) for i in range(final)] + [(t, final) for t in range(LAST, 0, -1)]:
             nc.vector.tensor_copy(window[t][:, quarters[i]].unsqueeze(1), h_rows(i, slice(t, t + 1)))
 
         gate = tile([P, PACK, H], F32, "gate")
@@ -275,27 +287,21 @@ def tile_picked_tokkerngate_none_po_kernel(
         def packed(c):
             return res_bf[:, c.start * PACK : c.stop * PACK]
 
-        def fetch_first(i):
-            nc.vector.tensor_copy(gate[:, 0, quarters[i]], window[0][:].indirect(entries(quarters[i])))
-
         def gated(i, rows):
             nc.vector.tensor_tensor(res[:, rows, quarters[i]], h_rows(i, rows), gate[:, rows, quarters[i]], ALU.mult)
 
-        def weave(i):
-            nc.vector.tensor_copy(woven(packed(quarters[i])), planar(res[:, :, quarters[i]]))
-
-        def planes(c):
+        def quantise_result(c):
             nc.vector.quantize_mx(out=res_codes[:, c].bitcast(FP8X4), scales=res_scales[:, c], in_=packed(c))
             nc.sync.dma_start(out_words[:, c], res_codes[:, c])
 
         for c in quarters:
             for t in range(1, PACK):
                 nc.scalar.activation(gate[:, t, c], window[t][:].indirect(entries(c)), ACT.Sigmoid)
-        for i in range(4):
-            fetch_first(i)
-        for i in range(3):
-            gated(i, slice(0, PACK))
-            if i < 2:
+        for c in quarters:
+            nc.vector.tensor_copy(gate[:, 0, c], window[0][:].indirect(entries(c)))
+        for i in range(final):
+            gated(i, every)
+            if i < final - 1:
                 nc.gpsimd.tensor_copy(
                     packed(quarters[i]).rearrange("p (c t) -> p c t", t=PACK),
                     res[:, :, quarters[i]].rearrange("p t c -> p c t"),
@@ -305,15 +311,13 @@ def tile_picked_tokkerngate_none_po_kernel(
             if i > 0:
                 c = halves[0] if i == 1 else quarters[i]
                 nc.sync.dma_start(out_rows[:, :, c], res[:, :, c])
-        gated(3, slice(0, 1))
-        gated(3, slice(1, last))
-        planes(halves[0])
-        gated(3, late)
-        nc.sync.dma_start(out_rows[:, :, quarters[3]], res[:, :, quarters[3]])
-        weave(3)
-        planes(halves[1])
-        for q in range(4):
+        gated(final, slice(0, 1))
+        gated(final, slice(1, LAST))
+        quantise_result(halves[0])
+        gated(final, late)
+        nc.sync.dma_start(out_rows[:, :, quarters[final]], res[:, :, quarters[final]])
+        nc.vector.tensor_copy(woven(packed(quarters[final])), planar(res[:, :, quarters[final]]))
+        quantise_result(halves[1])
+        for q in range(QUADS):
             queue = nc.sync if q % 2 == 0 else nc.scalar
-            queue.dma_start(
-                out_2[0, 4 * q : 4 * q + 4, :].bitcast(I32), res_scales[32 * q : 32 * q + 4, :].bitcast(I32)
-            )
+            queue.dma_start(hbm_rows(out_2, q), live_rows(res_scales, q))

from contextlib import ExitStack

import concourse.mybir as mybir
from concourse.masks import make_identity

K, T, S, N, H = 512, 2048, 512, 512, 512
FLOPS = 2 * K * S * H + 2 * S * N * H

F32 = mybir.dt.float32
BF16 = mybir.dt.bfloat16
I32 = mybir.dt.int32
U32 = mybir.dt.uint32
U16 = mybir.dt.uint16
U8 = mybir.dt.uint8
FP8X4 = mybir.dt.float8_e4m3fn_x4
FP4X4 = mybir.dt.float4_e2m1fn_x4
ACT = mybir.ActivationFunctionType
ALU = mybir.AluOpType

P = 128
PACK = 4
LAST = PACK - 1
HALF = H // 2
PARTS = H // P
LANES = 16
QUADS = 4
RUN = 4


def tile_picked_tokkerngate_none_po_kernel(
    tc, x_words, x_scales, wa, gt, w1_words, w1_scales, offs, n1, n2, n3, out_0, out_1, out_2
):
    nc = tc.nc
    halves = [slice(h * HALF, (h + 1) * HALF) for h in range(2)]
    quarters = [slice(i * P, (i + 1) * P) for i in range(PARTS)]
    all_cols = slice(0, H)
    early, late, every = slice(0, LAST), slice(LAST, PACK), slice(0, PACK)

    def live_rows(plane, q):
        return plane[32 * q : 32 * q + 4, :].bitcast(I32)

    def hbm_rows(scales, q):
        return scales[0, 4 * q : 4 * q + 4, :].bitcast(I32)

    def woven(ap):
        return ap.rearrange("p (c i t) -> p c t i", i=RUN, t=PACK)

    def planar(ap):
        return ap.rearrange("p t (c i) -> p c t i", i=RUN)

    with ExitStack() as ctx:
        sb = ctx.enter_context(tc.tile_pool(name="sb", bufs=1))
        ps = ctx.enter_context(tc.psum_pool(name="ps", bufs=1))

        def tile(shape, dtype, name, tag=""):
            return sb.tile(shape, dtype, name=name, tag=tag or name, align_bytes=64)

        offs_sb = tile([P, S // LANES], U16, "offs_sb")
        n1_sb = tile([P, H // LANES], U16, "n1_sb")
        n2_sb = tile([P, H // LANES], U16, "n2_sb")
        n3_sb = tile([P, H // LANES], U16, "n3_sb")
        xw_all = tile([P, T], I32, "xw_all")
        xs_all = tile([P, T], U8, "xs_all")
        w1w_raw = tile([P, 2 * N], U8, "w1w_raw")
        w1s_raw = tile([P, N], U8, "w1s_raw")
        wa_cuts = [halves[0], quarters[2], quarters[3]]
        wa_raw = [tile([P, PACK, c.stop - c.start], F32, f"wa_raw{c.start}") for c in wa_cuts]
        gt_sb = tile([P, PACK], F32, "gt_sb")

        nc.vector.memset(xs_all[:].bitcast(I32), 0)
        nc.vector.memset(w1s_raw[:].bitcast(I32), 0)
        y_wide = [tile([P, 2 * H], F32, f"y_wide{t}") for t in range(PACK)]
        y_sb = [wide[:, :H] for wide in y_wide]
        for wide in y_wide:
            nc.vector.memset(wide[:, H:], 0.0)

        nc.sync.dma_start(offs_sb[:], offs)
        for q in range(QUADS):
            nc.sync.dma_start(live_rows(xs_all, q), hbm_rows(x_scales, q))
        wa_rows = wa.rearrange("(p j) c -> p j c", j=PACK)
        nc.sync.dma_start(wa_raw[0][:], wa_rows[:, :, wa_cuts[0]])
        nc.sync.dma_start(xw_all[:], x_words[0].rearrange("p c r -> p (c r)").bitcast(I32))
        for raw, c in zip(wa_raw[1:], wa_cuts[1:]):
            nc.sync.dma_start(raw[:], wa_rows[:, :, c])
        nc.sync.dma_start(n1_sb[:], n1)
        nc.sync.dma_start(n2_sb[:], n2)
        nc.sync.dma_start(w1w_raw[:].bitcast(I32), w1_words[0].bitcast(I32))
        for q in range(QUADS):
            nc.sync.dma_start(live_rows(w1s_raw, q), hbm_rows(w1_scales, q))
        nc.sync.dma_start(gt_sb[:], gt.rearrange("(p t) o -> p (t o)", t=PACK))
        nc.sync.dma_start(n3_sb[:], n3)

        xs_picked = tile([P, S], U8, "xs_picked")
        xs_dealt = tile([P, S], U8, "xs_dealt")
        xw_dealt = tile([P, S], U32, "xw_dealt")
        nc.vector.tensor_copy(xs_picked[:], xs_all[:].indirect(offs_sb[:]))
        nc.vector.tensor_copy(
            xs_dealt[:].rearrange("p (t m) -> p t m", t=PACK), xs_picked[:].rearrange("p (m t) -> p t m", t=PACK)
        )
        nc.vector.tensor_copy(
            xw_dealt[:].rearrange("p (t m) -> p m t", t=PACK), xw_all[:].bitcast(U32).indirect(offs_sb[:])
        )

        wa_bf = [tile([P, (c.stop - c.start) * PACK], BF16, f"wa_bf{c.start}") for c in wa_cuts]
        wa_codes = tile([P, H], U32, "wa_codes")
        wa_scales = tile([P, H], U8, "wa_scales")
        y_ps = [ps.tile([P, H], F32, name=f"y_ps{t}", tag=f"bank{t}") for t in range(PACK)]
        y_early = ps.tile([P, HALF], F32, name="y_early", tag="spare")
        for i, c in enumerate(wa_cuts):
            if i < len(wa_cuts) - 1:
                nc.scalar.copy(woven(wa_bf[i][:]), planar(wa_raw[i][:]))
            else:
                nc.vector.tensor_copy(woven(wa_bf[i][:]), planar(wa_raw[i][:]))
            nc.vector.quantize_mx(out=wa_codes[:, c].bitcast(FP8X4), scales=wa_scales[:, c], in_=wa_bf[i][:])
        for t in range(PACK):
            tokens = slice(t * P, (t + 1) * P)
            for c in wa_cuts:
                nc.tensor.matmul_mx(
                    out=y_early[:] if t == 0 and c == halves[0] else y_ps[t][:, c],
                    lhsT=xw_dealt[:, tokens].bitcast(FP8X4),
                    lhsT_scale=xs_dealt[:, tokens],
                    rhs=wa_codes[:, c].bitcast(FP8X4),
                    rhs_scale=wa_scales[:, c],
                    start=True,
                    stop=True,
                )

        ident = tile([P, P], F32, "ident")
        make_identity(nc, ident[:])
        w1w_dealt = tile([P, 2 * N], U8, "w1w_dealt", tag=f"wa_bf{wa_cuts[-1].start}")
        nc.gpsimd.tensor_copy(
            w1w_dealt[:].rearrange("p (t m b) -> p t m b", t=PACK, b=2),
            w1w_raw[:].rearrange("p (m t b) -> p t m b", t=PACK, b=2),
        )

        near = [tile([P, 2, H], F32, f"near{t}") for t in range(PACK)]
        diff_all = tile([P, PACK + 1, 2, H], F32, "diff_all")
        diff = [diff_all[:, t, :, :] for t in range(PACK)]
        sq = [tile([P, 2, H], F32, f"sq{t}") for t in range(PACK)]
        kern = [tile([P, 2, H], F32, f"kern{t}") for t in range(PACK)]
        prod = tile([P, PACK, 2, H], F32, "prod")
        den_sq = diff_all[:, 1:, 1, :]
        num = tile([P, PACK, H], F32, "num")

        nc.scalar.copy(y_sb[0][:, halves[0]], y_early[:])
        nc.scalar.copy(y_sb[0][:, halves[1]], y_ps[0][:, halves[1]])
        for t in range(1, PACK):
            nc.scalar.copy(y_sb[t], y_ps[t][:])

        def kernel_sum(t):
            den_ps = ps.tile([P, H], F32, name="den_ps", tag="den_ps", bufs=2)
            for c in quarters:
                for e in range(2):
                    nc.tensor.matmul(
                        den_ps[:, c], kern[t][:, e, c], ident[:], start=e == 0, stop=e == 1, is_transpose=True
                    )
            return den_ps

        def square(t, den_ps, c):
            nc.scalar.activation(den_sq[:, t, c], den_ps[:, c], ACT.Square, bias=0.5)

        for t in range(PACK):
            for e, lst in enumerate((n1_sb, n2_sb)):
                nc.vector.tensor_copy(near[t][:, e, :], y_wide[t][:].indirect(lst[:]))
            for e in range(2):
                if t < LAST:
                    nc.gpsimd.tensor_tensor(diff[t][:, e, :], y_sb[t], near[t][:, e, :], ALU.subtract)
                elif e == 0:
                    low, high = halves
                    nc.vector.tensor_tensor(diff[t][:, e, high], y_ps[t][:, high], near[t][:, e, high], ALU.subtract)
                    nc.gpsimd.tensor_tensor(diff[t][:, e, low], y_sb[t][:, low], near[t][:, e, low], ALU.subtract)
                else:
                    nc.vector.tensor_tensor(diff[t][:, e, :], y_ps[t][:], near[t][:, e, :], ALU.subtract)
                for c in reversed(halves):
                    nc.scalar.activation(sq[t][:, e, c], diff[t][:, e, c], ACT.Square)
                for c in reversed(halves):
                    nc.scalar.activation(kern[t][:, e, c], sq[t][:, e, c], ACT.Exp, scale=-0.5)
            if t > 0:
                square(t - 1, kernel_sum(t - 1), all_cols)

        inv_t = [sq[LAST][:].rearrange("p e (u c) -> p (e u) c", u=2), den_sq[:, :, halves[0]]]

        def invert(rows, c):
            h = c.start // HALF
            inner = slice(c.start - h * HALF, c.stop - h * HALF)
            nc.scalar.activation(inv_t[h][:, rows, inner], den_sq[:, rows, c], ACT.Abs_reciprocal_sqrt)

        inv_ps = []

        def turn_back(i):
            inv_ps.append(ps.tile([P, PACK, P], F32, name=f"inv_ps{i}", tag=f"bank{i}"))
            for t in range(PACK):
                nc.tensor.transpose(inv_ps[i][:, t, :], inv_t[i // 2][:, t, quarters[i % 2]], ident[:])

        den_last = kernel_sum(LAST)
        invert(early, quarters[0])
        square(LAST, den_last, halves[0])
        invert(early, quarters[1])
        invert(late, halves[0])
        turn_back(0)
        turn_back(1)
        square(LAST, den_last, halves[1])
        invert(early, quarters[2])
        invert(late, quarters[2])
        turn_back(2)
        invert(every, quarters[3])
        turn_back(3)

        def products(t, c):
            nc.vector.scalar_tensor_tensor(
                prod[:, t, :, c], kern[t][:, :, c], gt_sb[:, t : t + 1], near[t][:, :, c], ALU.mult, ALU.mult
            )

        def numerator(rows):
            nc.vector.tensor_tensor(num[:, rows, :], prod[:, rows, 0, :], prod[:, rows, 1, :], ALU.add)

        for t in range(LAST):
            products(t, all_cols)
        numerator(slice(0, LAST - 1))
        for c in halves:
            products(LAST, c)
        numerator(slice(LAST - 1, LAST))
        numerator(late)

        w1s_dealt = tile([P, N], U8, "w1s_dealt", tag="prod")
        nc.gpsimd.tensor_copy(
            w1s_dealt[:].rearrange("p (t m) -> p t m", t=PACK), w1s_raw[:].rearrange("p (m t) -> p t m", t=PACK)
        )

        z_bf = [tile([P, P * PACK], BF16, f"z_bf{i}") for i in range(PARTS)]
        z_codes = tile([P, H], U32, "z_codes")
        z_scales = tile([P, H], U8, "z_scales")
        final = PARTS - 1
        h_ps = []
        h_late = ps.tile([P, PACK, P], F32, name="h_late", tag="spare")
        window = {t: tile([P, H], F32, f"window{t}") for t in (0, 1, 3)}

        def divide(i):
            c = quarters[i]
            nc.vector.tensor_tensor(woven(z_bf[i][:]), planar(inv_ps[i][:]), planar(num[:, :, c]), ALU.mult)

        def h_rows(i, rows):
            return (h_late if i == final and rows.start >= 1 else h_ps[i])[:, rows, :]

        def second_product(i):
            c = quarters[i]
            nc.vector.quantize_mx(out=z_codes[:, c].bitcast(FP8X4), scales=z_scales[:, c], in_=z_bf[i][:])
            h_ps.append(ps.tile([P, PACK, P], F32, name=f"h_ps{i}", tag=f"bank{i}"))
            for t in range(PACK):
                nc.tensor.matmul_mx(
                    out=h_late[:, t, :] if i == final and t >= 1 else h_ps[i][:, t, :],
                    lhsT=w1w_dealt[:, 2 * t * P : 2 * (t + 1) * P].bitcast(FP4X4),
                    lhsT_scale=w1s_dealt[:, t * P : (t + 1) * P],
                    rhs=z_codes[:, c].bitcast(FP8X4),
                    rhs_scale=z_scales[:, c],
                    start=True,
                    stop=True,
                )
            if i == final - 1:
                for t in (1, 3):
                    nc.vector.tensor_copy(window[t][:, c], h_ps[i][:, t, :])
            nc.scalar.activation(window[0][:, c], h_ps[i][:, 0, :], ACT.Sigmoid)
            if i < final - 1:
                for t in (1, 3):
                    nc.scalar.copy(window[t][:, c], h_ps[i][:, t, :])

        divide(0)
        for i in range(1, PARTS):
            divide(i)
            second_product(i - 1)
        second_product(final)
        window.setdefault(2, tile([P, H], F32, "window2", tag="num"))
        for t, i in [(2, i) for i in range(final)] + [(t, final) for t in range(LAST, 0, -1)]:
            nc.vector.tensor_copy(window[t][:, quarters[i]].unsqueeze(1), h_rows(i, slice(t, t + 1)))

        gate = tile([P, PACK, H], F32, "gate")
        res = tile([P, PACK, H], F32, "res")
        res_bf = tile([P, H * PACK], BF16, "res_bf")
        res_codes = tile([P, H], I32, "res_codes")
        res_scales = tile([P, H], U8, "res_scales")
        out_rows = out_0.rearrange("(p t) c -> p t c", t=PACK)
        out_words = out_1[0].rearrange("p c r -> p (c r)").bitcast(I32)

        def entries(c):
            return n3_sb[:, c.start // LANES : c.stop // LANES]

        def packed(c):
            return res_bf[:, c.start * PACK : c.stop * PACK]

        def gated(i, rows):
            nc.vector.tensor_tensor(res[:, rows, quarters[i]], h_rows(i, rows), gate[:, rows, quarters[i]], ALU.mult)

        def quantise_result(c):
            nc.vector.quantize_mx(out=res_codes[:, c].bitcast(FP8X4), scales=res_scales[:, c], in_=packed(c))
            nc.sync.dma_start(out_words[:, c], res_codes[:, c])

        for c in quarters:
            for t in range(1, PACK):
                nc.scalar.activation(gate[:, t, c], window[t][:].indirect(entries(c)), ACT.Sigmoid)
        for c in quarters:
            nc.vector.tensor_copy(gate[:, 0, c], window[0][:].indirect(entries(c)))
        for i in range(final):
            gated(i, every)
            if i < final - 1:
                nc.gpsimd.tensor_copy(
                    packed(quarters[i]).rearrange("p (c t) -> p c t", t=PACK),
                    res[:, :, quarters[i]].rearrange("p t c -> p c t"),
                )
            else:
                nc.scalar.copy(woven(packed(quarters[i])), planar(res[:, :, quarters[i]]))
            if i > 0:
                c = halves[0] if i == 1 else quarters[i]
                nc.sync.dma_start(out_rows[:, :, c], res[:, :, c])
        gated(final, slice(0, 1))
        gated(final, slice(1, LAST))
        quantise_result(halves[0])
        gated(final, late)
        nc.sync.dma_start(out_rows[:, :, quarters[final]], res[:, :, quarters[final]])
        nc.vector.tensor_copy(woven(packed(quarters[final])), planar(res[:, :, quarters[final]]))
        quantise_result(halves[1])
        for q in range(QUADS):
            queue = nc.sync if q % 2 == 0 else nc.scalar
            queue.dma_start(hbm_rows(out_2, q), live_rows(res_scales, q))
